import numpy as np
import ml_dtypes

BF16 = ml_dtypes.bfloat16


def bf(x):
    return np.asarray(x, np.float32).astype(BF16)


def f32(x):
    return np.asarray(x, np.float32)


def f64(x):
    return np.asarray(x).astype(np.float64)


def striped(idx):
    return np.tile(idx.reshape(-1, 16).T, (8, 1))


S, K, M, N, E, Q = 512, 128, 256, 512, 2, 256


def gelu_tanh(v):
    return 0.5 * v * (1.0 + np.tanh(np.sqrt(2.0 / np.pi) * (v + 0.044715 * v**3)))


def setup_inputs():
    return {"base": bf(np.random.standard_normal((M, S))), "x": bf(np.random.standard_normal((K, N))), "w": bf(np.random.standard_normal((E, K, M)) / np.sqrt(K)), "b": f32(0.5 * np.random.standard_normal((M, 1))), "offs": striped(np.random.permutation(S))}


def reference(base, x, w, b, offs):
    idx = offs[:16].T.reshape(-1)
    z = f64(base).copy()
    for e in range(E):
        z[:, idx[e * Q : (e + 1) * Q]] += f64(w)[e].T @ f64(x)[:, e * Q : (e + 1) * Q]
    return gelu_tanh(z + f64(b))

@@ -1,0 +1,59 @@
+import concourse.mybir as mybir
+from concourse.masks import make_identity
+
+BF16, F32, U16 = mybir.dt.bfloat16, mybir.dt.float32, mybir.dt.uint16
+GELU = mybir.ActivationFunctionType.Gelu_apprx_tanh
+
+P = 128
+TOKENS = 512
+FEATURES = 256
+BLOCKS = FEATURES // P
+EXPERTS = 2
+PIECE = 256
+PIECE_COLS = PIECE // 16
+
+FLOPS = 2 * P * FEATURES * EXPERTS * PIECE
+
+
+def tile_scatter_matmul_kernel(tc, base, x, w, b, offs, out):
+    nc = tc.nc
+    with (
+        tc.tile_pool(name="held", bufs=1) as held,
+        tc.psum_pool(name="banks", bufs=1) as banks,
+    ):
+        offsets = held.tile([P, EXPERTS * PIECE_COLS], U16, name="offsets")
+        nc.sync.dma_start(offsets[:], offs)
+
+        base_rows = [held.tile([P, TOKENS], BF16, name=f"base_rows{a}") for a in range(BLOCKS)]
+        nc.sync.dma_start(base_rows[0][:], base[0:P, :])
+        nc.scalar.dma_start(base_rows[1][:], base[P : 2 * P, :])
+        weights = [held.tile([P, FEATURES], BF16, name=f"weights{e}") for e in range(EXPERTS)]
+        nc.sync.dma_start(weights[0][:], w[0])
+        nc.scalar.dma_start(weights[1][:], w[1])
+        moving = held.tile([P, EXPERTS * PIECE], BF16, name="moving")
+        nc.sync.dma_start(moving[:], x)
+        bias = held.tile([P, BLOCKS], F32, name="bias")
+        with nc.allow_non_contiguous_dma(reason="one float32 to a partition for each block of features"):
+            nc.scalar.dma_start(bias[:], b.rearrange("(a p) o -> p (a o)", p=P))
+
+        ident = held.tile([P, P], BF16, name="ident")
+        make_identity(nc, ident[:])
+
+        windows = [banks.tile([P, TOKENS], F32, name=f"window{a}") for a in range(BLOCKS)]
+        for a in range(BLOCKS):
+            nc.tensor.matmul(windows[a][:], ident[:], base_rows[a][:], start=True, stop=False)
+
+        for a in range(BLOCKS):
+            for e in range(EXPERTS):
+                nc.tensor.matmul(
+                    windows[a][:].indirect(offsets[:, e * PIECE_COLS : (e + 1) * PIECE_COLS]),
+                    weights[e][:, a * P : (a + 1) * P],
+                    moving[:, e * PIECE : (e + 1) * PIECE],
+                    start=False,
+                    stop=(e == EXPERTS - 1),
+                )
+
+        for a in range(BLOCKS):
+            result = held.tile([P, TOKENS], F32, name=f"result{a}")
+            nc.scalar.activation(result[:], windows[a][:], GELU, bias=bias[:, a : a + 1])
+            nc.sync.dma_start(out[a * P : (a + 1) * P, :], result[:])

@@ -12,6 +12,8 @@ EXPERTS = 2
 PIECE = 256
 PIECE_COLS = PIECE // 16
 
+WARM_UPS = 12
+
 FLOPS = 2 * P * FEATURES * EXPERTS * PIECE
 
 
@@ -21,23 +23,29 @@ def tile_scatter_matmul_kernel(tc, base, x, w, b, offs, out):
         tc.tile_pool(name="held", bufs=1) as held,
         tc.psum_pool(name="banks", bufs=1) as banks,
     ):
+        base_rows = [held.tile([P, TOKENS], BF16, name=f"base_rows{a}") for a in range(BLOCKS)]
+        for a in range(BLOCKS):
+            nc.sync.dma_start(base_rows[a][:], base[a * P : (a + 1) * P, :])
         offsets = held.tile([P, EXPERTS * PIECE_COLS], U16, name="offsets")
         nc.sync.dma_start(offsets[:], offs)
-
-        base_rows = [held.tile([P, TOKENS], BF16, name=f"base_rows{a}") for a in range(BLOCKS)]
-        nc.sync.dma_start(base_rows[0][:], base[0:P, :])
-        nc.scalar.dma_start(base_rows[1][:], base[P : 2 * P, :])
-        weights = [held.tile([P, FEATURES], BF16, name=f"weights{e}") for e in range(EXPERTS)]
-        nc.sync.dma_start(weights[0][:], w[0])
-        nc.scalar.dma_start(weights[1][:], w[1])
+        weights = held.tile([P, EXPERTS, FEATURES], BF16, name="weights")
+        nc.sync.dma_start(weights[:], w.rearrange("e k m -> k e m"))
         moving = held.tile([P, EXPERTS * PIECE], BF16, name="moving")
         nc.sync.dma_start(moving[:], x)
+
+        ident = held.tile([P, P], BF16, name="ident")
+        make_identity(nc, ident[:])
         bias = held.tile([P, BLOCKS], F32, name="bias")
         with nc.allow_non_contiguous_dma(reason="one float32 to a partition for each block of features"):
             nc.scalar.dma_start(bias[:], b.rearrange("(a p) o -> p (a o)", p=P))
 
-        ident = held.tile([P, P], BF16, name="ident")
-        make_identity(nc, ident[:])
+        zeros = held.tile([P, P], BF16, name="zeros")
+        nc.vector.memset(zeros[:], 0.0)
+        unused = held.tile([P, 1], F32, name="unused")
+        nc.scalar.activation(unused[:], zeros[:, 0:1], GELU)
+        spare_bank = banks.tile([P, P], F32, name="spare_bank")
+        for i in range(WARM_UPS):
+            nc.tensor.matmul(spare_bank[:], zeros[:], zeros[:], start=True, stop=True)
 
         windows = [banks.tile([P, TOKENS], F32, name=f"window{a}") for a in range(BLOCKS)]
         for a in range(BLOCKS):
@@ -47,7 +55,7 @@ def tile_scatter_matmul_kernel(tc, base, x, w, b, offs, out):
             for e in range(EXPERTS):
                 nc.tensor.matmul(
                     windows[a][:].indirect(offsets[:, e * PIECE_COLS : (e + 1) * PIECE_COLS]),
-                    weights[e][:, a * P : (a + 1) * P],
+                    weights[:, e, a * P : (a + 1) * P],
                     moving[:, e * PIECE : (e + 1) * PIECE],
                     start=False,
                     stop=(e == EXPERTS - 1),

@@ -32,12 +32,12 @@ def tile_scatter_matmul_kernel(tc, base, x, w, b, offs, out):
         nc.sync.dma_start(weights[:], w.rearrange("e k m -> k e m"))
         moving = held.tile([P, EXPERTS * PIECE], BF16, name="moving")
         nc.sync.dma_start(moving[:], x)
+        bias = held.tile([P, BLOCKS], F32, name="bias")
+        with nc.allow_non_contiguous_dma(reason="one float32 to a partition for each block of features"):
+            nc.sync.dma_start(bias[:], b.rearrange("(a p) o -> p (a o)", p=P))
 
         ident = held.tile([P, P], BF16, name="ident")
         make_identity(nc, ident[:])
-        bias = held.tile([P, BLOCKS], F32, name="bias")
-        with nc.allow_non_contiguous_dma(reason="one float32 to a partition for each block of features"):
-            nc.scalar.dma_start(bias[:], b.rearrange("(a p) o -> p (a o)", p=P))
 
         zeros = held.tile([P, P], BF16, name="zeros")
         nc.vector.memset(zeros[:], 0.0)
@@ -62,6 +62,10 @@ def tile_scatter_matmul_kernel(tc, base, x, w, b, offs, out):
                 )
 
         for a in range(BLOCKS):
-            result = held.tile([P, TOKENS], F32, name=f"result{a}")
-            nc.scalar.activation(result[:], windows[a][:], GELU, bias=bias[:, a : a + 1])
-            nc.sync.dma_start(out[a * P : (a + 1) * P, :], result[:])
+            halves = 2 if a == BLOCKS - 1 else 1
+            width = TOKENS // halves
+            for h in range(halves):
+                columns = slice(h * width, (h + 1) * width)
+                result = held.tile([P, width], F32, name=f"result{a}_{h}")
+                nc.scalar.activation(result[:], windows[a][:, columns], GELU, bias=bias[:, a : a + 1])
+                nc.sync.dma_start(out[a * P : (a + 1) * P, columns], result[:])

@@ -28,10 +28,11 @@ def tile_scatter_matmul_kernel(tc, base, x, w, b, offs, out):
             nc.sync.dma_start(base_rows[a][:], base[a * P : (a + 1) * P, :])
         offsets = held.tile([P, EXPERTS * PIECE_COLS], U16, name="offsets")
         nc.sync.dma_start(offsets[:], offs)
-        weights = held.tile([P, EXPERTS, FEATURES], BF16, name="weights")
-        nc.sync.dma_start(weights[:], w.rearrange("e k m -> k e m"))
-        moving = held.tile([P, EXPERTS * PIECE], BF16, name="moving")
-        nc.sync.dma_start(moving[:], x)
+        weights = [held.tile([P, FEATURES], BF16, name=f"weights{e}") for e in range(EXPERTS)]
+        moving = [held.tile([P, PIECE], BF16, name=f"moving{e}") for e in range(EXPERTS)]
+        for e in range(EXPERTS):
+            nc.sync.dma_start(weights[e][:], w[e])
+            nc.sync.dma_start(moving[e][:], x[:, e * PIECE : (e + 1) * PIECE])
         bias = held.tile([P, BLOCKS], F32, name="bias")
         with nc.allow_non_contiguous_dma(reason="one float32 to a partition for each block of features"):
             nc.sync.dma_start(bias[:], b.rearrange("(a p) o -> p (a o)", p=P))
@@ -55,8 +56,8 @@ def tile_scatter_matmul_kernel(tc, base, x, w, b, offs, out):
             for e in range(EXPERTS):
                 nc.tensor.matmul(
                     windows[a][:].indirect(offsets[:, e * PIECE_COLS : (e + 1) * PIECE_COLS]),
-                    weights[:, e, a * P : (a + 1) * P],
-                    moving[:, e * PIECE : (e + 1) * PIECE],
+                    weights[e][:, a * P : (a + 1) * P],
+                    moving[e][:],
                     start=False,
                     stop=(e == EXPERTS - 1),
                 )

@@ -12,6 +12,7 @@ EXPERTS = 2
 PIECE = 256
 PIECE_COLS = PIECE // 16
 
+HALVES = 2
 WARM_UPS = 12
 
 FLOPS = 2 * P * FEATURES * EXPERTS * PIECE
@@ -62,10 +63,9 @@ def tile_scatter_matmul_kernel(tc, base, x, w, b, offs, out):
                     stop=(e == EXPERTS - 1),
                 )
 
+        width = TOKENS // HALVES
         for a in range(BLOCKS):
-            halves = 2 if a == BLOCKS - 1 else 1
-            width = TOKENS // halves
-            for h in range(halves):
+            for h in range(HALVES):
                 columns = slice(h * width, (h + 1) * width)
                 result = held.tile([P, width], F32, name=f"result{a}_{h}")
                 nc.scalar.activation(result[:], windows[a][:, columns], GELU, bias=bias[:, a : a + 1])

@@ -12,6 +12,7 @@ EXPERTS = 2
 PIECE = 256
 PIECE_COLS = PIECE // 16
 
+BURST = 256
 HALVES = 2
 WARM_UPS = 12
 
@@ -24,13 +25,13 @@ def tile_scatter_matmul_kernel(tc, base, x, w, b, offs, out):
         tc.tile_pool(name="held", bufs=1) as held,
         tc.psum_pool(name="banks", bufs=1) as banks,
     ):
-        base_rows = [held.tile([P, TOKENS], BF16, name=f"base_rows{a}") for a in range(BLOCKS)]
+        base_rows = [held.tile([P, TOKENS], BF16, name=f"base_rows{a}", align_bytes=BURST) for a in range(BLOCKS)]
         for a in range(BLOCKS):
             nc.sync.dma_start(base_rows[a][:], base[a * P : (a + 1) * P, :])
         offsets = held.tile([P, EXPERTS * PIECE_COLS], U16, name="offsets")
         nc.sync.dma_start(offsets[:], offs)
-        weights = [held.tile([P, FEATURES], BF16, name=f"weights{e}") for e in range(EXPERTS)]
-        moving = [held.tile([P, PIECE], BF16, name=f"moving{e}") for e in range(EXPERTS)]
+        weights = [held.tile([P, FEATURES], BF16, name=f"weights{e}", align_bytes=BURST) for e in range(EXPERTS)]
+        moving = [held.tile([P, PIECE], BF16, name=f"moving{e}", align_bytes=BURST) for e in range(EXPERTS)]
         for e in range(EXPERTS):
             nc.sync.dma_start(weights[e][:], w[e])
             nc.sync.dma_start(moving[e][:], x[:, e * PIECE : (e + 1) * PIECE])
@@ -67,6 +68,6 @@ def tile_scatter_matmul_kernel(tc, base, x, w, b, offs, out):
         for a in range(BLOCKS):
             for h in range(HALVES):
                 columns = slice(h * width, (h + 1) * width)
-                result = held.tile([P, width], F32, name=f"result{a}_{h}")
+                result = held.tile([P, width], F32, name=f"result{a}_{h}", align_bytes=BURST)
                 nc.scalar.activation(result[:], windows[a][:, columns], GELU, bias=bias[:, a : a + 1])
                 nc.sync.dma_start(out[a * P : (a + 1) * P, columns], result[:])

@@ -14,7 +14,9 @@ PIECE_COLS = PIECE // 16
 
 BURST = 256
 HALVES = 2
-WARM_UPS = 12
+COLUMN_TILE = 32
+WARM_UP_ROUNDS = 2
+REPEATS = TOKENS // P
 
 FLOPS = 2 * P * FEATURES * EXPERTS * PIECE
 
@@ -46,9 +48,17 @@ def tile_scatter_matmul_kernel(tc, base, x, w, b, offs, out):
         nc.vector.memset(zeros[:], 0.0)
         unused = held.tile([P, 1], F32, name="unused")
         nc.scalar.activation(unused[:], zeros[:, 0:1], GELU)
-        spare_bank = banks.tile([P, P], F32, name="spare_bank")
-        for i in range(WARM_UPS):
-            nc.tensor.matmul(spare_bank[:], zeros[:], zeros[:], start=True, stop=True)
+        spare_bank = banks.tile([P, TOKENS], F32, name="spare_bank")
+        zero_columns = zeros[:].unsqueeze(1).to_broadcast([P, REPEATS, P])
+        for i in range(WARM_UP_ROUNDS):
+            for first in range(0, P, COLUMN_TILE):
+                nc.tensor.matmul(
+                    spare_bank[first : first + COLUMN_TILE, :].rearrange("p (r c) -> p r c", r=REPEATS),
+                    zeros[:, 0:COLUMN_TILE],
+                    zero_columns,
+                    start=True,
+                    stop=True,
+                )
 
         windows = [banks.tile([P, TOKENS], F32, name=f"window{a}") for a in range(BLOCKS)]
         for a in range(BLOCKS):

@@ -17,6 +17,8 @@ HALVES = 2
 COLUMN_TILE = 32
 WARM_UP_ROUNDS = 2
 REPEATS = TOKENS // P
+SQUARE = 32
+QUADRANTS = P // SQUARE
 
 FLOPS = 2 * P * FEATURES * EXPERTS * PIECE
 
@@ -34,18 +36,26 @@ def tile_scatter_matmul_kernel(tc, base, x, w, b, offs, out):
         nc.sync.dma_start(offsets[:], offs)
         weights = [held.tile([P, FEATURES], BF16, name=f"weights{e}", align_bytes=BURST) for e in range(EXPERTS)]
         moving = [held.tile([P, PIECE], BF16, name=f"moving{e}", align_bytes=BURST) for e in range(EXPERTS)]
+        zeros = held.tile([P, P], BF16, name="zeros")
+        nc.vector.memset(zeros[:], 0.0)
+        bias_rows = held.tile([P, BLOCKS * SQUARE], F32, name="bias_rows", align_bytes=64)
+        nc.vector.memset(bias_rows[:], 0.0)
         for e in range(EXPERTS):
             nc.sync.dma_start(weights[e][:], w[e])
             nc.sync.dma_start(moving[e][:], x[:, e * PIECE : (e + 1) * PIECE])
-        bias = held.tile([P, BLOCKS], F32, name="bias")
-        with nc.allow_non_contiguous_dma(reason="one float32 to a partition for each block of features"):
-            nc.sync.dma_start(bias[:], b.rearrange("(a p) o -> p (a o)", p=P))
+            if e == 0:
+                nc.sync.dma_start(
+                    bias_rows[0:P:SQUARE, :].rearrange("q (a i) -> q a i", a=BLOCKS),
+                    b.rearrange("(a q i) o -> q a (i o)", a=BLOCKS, q=QUADRANTS),
+                )
+        bias = held.tile([P, BLOCKS * SQUARE], F32, name="bias", align_bytes=64)
+        for a in range(BLOCKS):
+            square = slice(a * SQUARE, (a + 1) * SQUARE)
+            nc.vector.transpose(bias[:, square], bias_rows[:, square])
 
         ident = held.tile([P, P], BF16, name="ident")
         make_identity(nc, ident[:])
 
-        zeros = held.tile([P, P], BF16, name="zeros")
-        nc.vector.memset(zeros[:], 0.0)
         unused = held.tile([P, 1], F32, name="unused")
         nc.scalar.activation(unused[:], zeros[:, 0:1], GELU)
         spare_bank = banks.tile([P, TOKENS], F32, name="spare_bank")
@@ -79,5 +89,5 @@ def tile_scatter_matmul_kernel(tc, base, x, w, b, offs, out):
             for h in range(HALVES):
                 columns = slice(h * width, (h + 1) * width)
                 result = held.tile([P, width], F32, name=f"result{a}_{h}", align_bytes=BURST)
-                nc.scalar.activation(result[:], windows[a][:, columns], GELU, bias=bias[:, a : a + 1])
+                nc.scalar.activation(result[:], windows[a][:, columns], GELU, bias=bias[:, a * SQUARE : a * SQUARE + 1])
                 nc.sync.dma_start(out[a * P : (a + 1) * P, columns], result[:])

@@ -34,20 +34,23 @@ def tile_scatter_matmul_kernel(tc, base, x, w, b, offs, out):
             nc.sync.dma_start(base_rows[a][:], base[a * P : (a + 1) * P, :])
         offsets = held.tile([P, EXPERTS * PIECE_COLS], U16, name="offsets")
         nc.sync.dma_start(offsets[:], offs)
-        weights = [held.tile([P, FEATURES], BF16, name=f"weights{e}", align_bytes=BURST) for e in range(EXPERTS)]
+        first_weights = [held.tile([P, P], BF16, name=f"first_weights{e}", align_bytes=BURST) for e in range(EXPERTS)]
+        later_weights = held.tile([P, EXPERTS, P], BF16, name="later_weights", align_bytes=BURST)
         moving = [held.tile([P, PIECE], BF16, name=f"moving{e}", align_bytes=BURST) for e in range(EXPERTS)]
         zeros = held.tile([P, P], BF16, name="zeros")
         nc.vector.memset(zeros[:], 0.0)
         bias_rows = held.tile([P, BLOCKS * SQUARE], F32, name="bias_rows", align_bytes=64)
         nc.vector.memset(bias_rows[:], 0.0)
         for e in range(EXPERTS):
-            nc.sync.dma_start(weights[e][:], w[e])
+            nc.sync.dma_start(first_weights[e][:], w[e][:, 0:P])
             nc.sync.dma_start(moving[e][:], x[:, e * PIECE : (e + 1) * PIECE])
             if e == 0:
                 nc.sync.dma_start(
                     bias_rows[0:P:SQUARE, :].rearrange("q (a i) -> q a i", a=BLOCKS),
                     b.rearrange("(a q i) o -> q a (i o)", a=BLOCKS, q=QUADRANTS),
                 )
+        nc.sync.dma_start(later_weights[:], w[:, :, P:FEATURES].rearrange("e k m -> k e m"))
+        weights = [[first_weights[e][:] for e in range(EXPERTS)], [later_weights[:, e, :] for e in range(EXPERTS)]]
         bias = held.tile([P, BLOCKS * SQUARE], F32, name="bias", align_bytes=64)
         for a in range(BLOCKS):
             square = slice(a * SQUARE, (a + 1) * SQUARE)
@@ -78,7 +81,7 @@ def tile_scatter_matmul_kernel(tc, base, x, w, b, offs, out):
             for e in range(EXPERTS):
                 nc.tensor.matmul(
                     windows[a][:].indirect(offsets[:, e * PIECE_COLS : (e + 1) * PIECE_COLS]),
-                    weights[e][:, a * P : (a + 1) * P],
+                    weights[a][e],
                     moving[e][:],
                     start=False,
                     stop=(e == EXPERTS - 1),

@@ -14,9 +14,7 @@ PIECE_COLS = PIECE // 16
 
 BURST = 256
 HALVES = 2
-COLUMN_TILE = 32
-WARM_UP_ROUNDS = 2
-REPEATS = TOKENS // P
+WARM_UPS = 12
 SQUARE = 32
 QUADRANTS = P // SQUARE
 
@@ -61,17 +59,9 @@ def tile_scatter_matmul_kernel(tc, base, x, w, b, offs, out):
 
         unused = held.tile([P, 1], F32, name="unused")
         nc.scalar.activation(unused[:], zeros[:, 0:1], GELU)
-        spare_bank = banks.tile([P, TOKENS], F32, name="spare_bank")
-        zero_columns = zeros[:].unsqueeze(1).to_broadcast([P, REPEATS, P])
-        for i in range(WARM_UP_ROUNDS):
-            for first in range(0, P, COLUMN_TILE):
-                nc.tensor.matmul(
-                    spare_bank[first : first + COLUMN_TILE, :].rearrange("p (r c) -> p r c", r=REPEATS),
-                    zeros[:, 0:COLUMN_TILE],
-                    zero_columns,
-                    start=True,
-                    stop=True,
-                )
+        spare_bank = banks.tile([P, P], F32, name="spare_bank")
+        for i in range(WARM_UPS):
+            nc.tensor.matmul(spare_bank[:], zeros[:], zeros[:], start=True, stop=True)
 
         windows = [banks.tile([P, TOKENS], F32, name=f"window{a}") for a in range(BLOCKS)]
         for a in range(BLOCKS):

@@ -14,7 +14,7 @@ PIECE_COLS = PIECE // 16
 
 BURST = 256
 HALVES = 2
-WARM_UPS = 12
+WARM_UPS = 9
 SQUARE = 32
 QUADRANTS = P // SQUARE
 

import concourse.mybir as mybir
from concourse.masks import make_identity

BF16, F32, U16 = mybir.dt.bfloat16, mybir.dt.float32, mybir.dt.uint16
GELU = mybir.ActivationFunctionType.Gelu_apprx_tanh

P = 128
TOKENS = 512
FEATURES = 256
BLOCKS = FEATURES // P
EXPERTS = 2
PIECE = 256
PIECE_COLS = PIECE // 16

BURST = 256
HALVES = 2
WARM_UPS = 9
SQUARE = 32
QUADRANTS = P // SQUARE

FLOPS = 2 * P * FEATURES * EXPERTS * PIECE


def tile_scatter_matmul_kernel(tc, base, x, w, b, offs, out):
    nc = tc.nc
    with (
        tc.tile_pool(name="held", bufs=1) as held,
        tc.psum_pool(name="banks", bufs=1) as banks,
    ):
        base_rows = [held.tile([P, TOKENS], BF16, name=f"base_rows{a}", align_bytes=BURST) for a in range(BLOCKS)]
        for a in range(BLOCKS):
            nc.sync.dma_start(base_rows[a][:], base[a * P : (a + 1) * P, :])
        offsets = held.tile([P, EXPERTS * PIECE_COLS], U16, name="offsets")
        nc.sync.dma_start(offsets[:], offs)
        first_weights = [held.tile([P, P], BF16, name=f"first_weights{e}", align_bytes=BURST) for e in range(EXPERTS)]
        later_weights = held.tile([P, EXPERTS, P], BF16, name="later_weights", align_bytes=BURST)
        moving = [held.tile([P, PIECE], BF16, name=f"moving{e}", align_bytes=BURST) for e in range(EXPERTS)]
        zeros = held.tile([P, P], BF16, name="zeros")
        nc.vector.memset(zeros[:], 0.0)
        bias_rows = held.tile([P, BLOCKS * SQUARE], F32, name="bias_rows", align_bytes=64)
        nc.vector.memset(bias_rows[:], 0.0)
        for e in range(EXPERTS):
            nc.sync.dma_start(first_weights[e][:], w[e][:, 0:P])
            nc.sync.dma_start(moving[e][:], x[:, e * PIECE : (e + 1) * PIECE])
            if e == 0:
                nc.sync.dma_start(
                    bias_rows[0:P:SQUARE, :].rearrange("q (a i) -> q a i", a=BLOCKS),
                    b.rearrange("(a q i) o -> q a (i o)", a=BLOCKS, q=QUADRANTS),
                )
        nc.sync.dma_start(later_weights[:], w[:, :, P:FEATURES].rearrange("e k m -> k e m"))
        weights = [[first_weights[e][:] for e in range(EXPERTS)], [later_weights[:, e, :] for e in range(EXPERTS)]]
        bias = held.tile([P, BLOCKS * SQUARE], F32, name="bias", align_bytes=64)
        for a in range(BLOCKS):
            square = slice(a * SQUARE, (a + 1) * SQUARE)
            nc.vector.transpose(bias[:, square], bias_rows[:, square])

        ident = held.tile([P, P], BF16, name="ident")
        make_identity(nc, ident[:])

        unused = held.tile([P, 1], F32, name="unused")
        nc.scalar.activation(unused[:], zeros[:, 0:1], GELU)
        spare_bank = banks.tile([P, P], F32, name="spare_bank")
        for i in range(WARM_UPS):
            nc.tensor.matmul(spare_bank[:], zeros[:], zeros[:], start=True, stop=True)

        windows = [banks.tile([P, TOKENS], F32, name=f"window{a}") for a in range(BLOCKS)]
        for a in range(BLOCKS):
            nc.tensor.matmul(windows[a][:], ident[:], base_rows[a][:], start=True, stop=False)

        for a in range(BLOCKS):
            for e in range(EXPERTS):
                nc.tensor.matmul(
                    windows[a][:].indirect(offsets[:, e * PIECE_COLS : (e + 1) * PIECE_COLS]),
                    weights[a][e],
                    moving[e][:],
                    start=False,
                    stop=(e == EXPERTS - 1),
                )

        width = TOKENS // HALVES
        for a in range(BLOCKS):
            for h in range(HALVES):
                columns = slice(h * width, (h + 1) * width)
                result = held.tile([P, width], F32, name=f"result{a}_{h}", align_bytes=BURST)
                nc.scalar.activation(result[:], windows[a][:, columns], GELU, bias=bias[:, a * SQUARE : a * SQUARE + 1])
                nc.sync.dma_start(out[a * P : (a + 1) * P, columns], result[:])
